import numpy as np
import ml_dtypes


def mxq(x, axis, fmt="e4m3"):
    dtype, down = {"e4m3": (ml_dtypes.float8_e4m3fn, 7), "e5m2": (ml_dtypes.float8_e5m2, 14)}[fmt]
    v = np.moveaxis(np.asarray(x, np.float32).astype(ml_dtypes.bfloat16).astype(np.float64), axis, -1)
    blocks = v.reshape(v.shape[:-1] + (-1, 32))
    amax = np.abs(blocks).max(-1, keepdims=True)
    byte = np.maximum(np.where(amax > 0, np.frexp(amax)[1] - 1 + 127, 0) - down, 1)
    scale = np.exp2(byte - 127.0)
    codes = (blocks / scale).astype(np.float32).astype(dtype).astype(np.float64)
    return np.moveaxis((codes * scale).reshape(v.shape), -1, axis)


WIDE = False


def mx_kscale(k):
    if not WIDE:
        return np.ones(k)
    levels = np.array([10, -10, 5, -5, 0])
    if k % 512:
        return np.exp2(np.random.permutation(np.resize(levels, k // 32))).repeat(32)
    a = np.empty((k // 512, 16))
    for p in range(k // 512):
        a[p, :8] = np.random.permutation(np.resize(levels, 8))
        for g in range(8):
            far = levels[np.abs(levels - a[p, g]) >= 10]
            a[p, g + 8] = far[np.random.randint(len(far))]
    return np.exp2(a.ravel()).repeat(32)


def f64(x):
    return np.asarray(x).astype(np.float64)


def striped(idx):
    return np.tile(np.asarray(idx).reshape(-1, 16).T, (8, 1)).astype(np.uint16)


def unstriped(offs):
    return offs[:16].T.reshape(-1).astype(np.int64)


E2M1 = np.array([0.0, 0.5, 1.0, 1.5, 2.0, 3.0, 4.0, 6.0, -0.0, -0.5, -1.0, -1.5, -2.0, -3.0, -4.0, -6.0])


def pack_weight(w, fmt):
    k, n = w.shape
    w = f64(np.asarray(w, np.float32).astype(ml_dtypes.bfloat16)).reshape(k // 32, 32, n)
    amax = np.abs(w).max(1)
    if fmt == "e4m3":
        byte = np.frexp(amax)[1] - 1 + 127 - 7
    else:
        mant, ex = np.frexp(amax / 6.0)
        byte = np.where(mant > 0.5, ex, ex - 1) + 127
    byte = np.clip(np.where(amax > 0, byte, 1), 1, 254)
    scaled = (w * np.exp2(127.0 - byte)[:, None, :]).reshape(k, n).astype(np.float32)
    by_word = np.ascontiguousarray(scaled.reshape(k // 512, 128, 4, n).transpose(0, 1, 3, 2))
    if fmt == "e4m3":
        words = by_word.astype(ml_dtypes.float8_e4m3fn).view(np.uint8)
    else:
        c = by_word.astype(ml_dtypes.float4_e2m1fn).view(np.uint8) & 0xF
        words = (c[..., 0::2] | (c[..., 1::2] << 4)).reshape(k // 512, 128, 2 * n)
    return np.ascontiguousarray(words), np.ascontiguousarray(byte.astype(np.uint8).reshape(k // 512, 16, n))


def unpack_weight(words, scales, fmt):
    g, _, n = scales.shape
    words = np.ascontiguousarray(words).reshape(g, 128, n, -1)
    if fmt == "e4m3":
        vals = words.view(ml_dtypes.float8_e4m3fn).astype(np.float64)
    else:
        nib = np.empty((g, 128, n, 4), np.uint8)
        nib[..., 0::2] = words & 0xF
        nib[..., 1::2] = words >> 4
        vals = E2M1[nib]
    vals = vals * np.repeat(np.exp2(scales.astype(np.float64) - 127.0), 8, axis=1)[..., None]
    return vals.transpose(0, 1, 3, 2).reshape(g * 512, n)


def bf(x):
    return np.asarray(x, np.float32).astype(ml_dtypes.bfloat16)


def planes(Y):
    r, m = Y.shape
    b = f64(bf(Y)).reshape(r // 32, 32, m)
    amax = np.abs(b).max(1)
    byte = np.clip(np.where(amax > 0, np.frexp(amax)[1] - 1 + 127 - 7, 1), 1, 254)
    codes = (b * np.exp2(127.0 - byte)[:, None, :]).reshape(r, m).astype(np.float32).astype(ml_dtypes.float8_e4m3fn).view(np.uint8)
    words = codes.reshape(r // 512, 128, 4, m).transpose(0, 1, 3, 2)
    return np.ascontiguousarray(words), np.ascontiguousarray(byte.astype(np.uint8).reshape(r // 512, 16, m))


D, T, I, Q, E, H, K = 512, 2048, 512, 256, 512, 32, 32


def setup_inputs():
    n = np.random.standard_normal
    idx = np.random.permutation(T)[:I]
    fd = mx_kscale(D)
    fi = mx_kscale(I)
    keysp = pack_weight(n((D, T)) / fd[:, None], "e2m1")
    return {
        "query": (n((D, Q)) * 1.0 / np.sqrt(D) * fd[:, None]).astype(np.float32),
        "keys_words": keysp[0],
        "keys_scales": keysp[1],
        "cv1": np.tile(np.random.uniform(0.3, 1.5, T), (128, 1)).astype(np.float32),
        "cv2": np.tile(np.random.uniform(-0.5, 0.3, T), (128, 1)).astype(np.float32),
        "sres": (np.random.uniform(1.0, 8.0, (I, 1))).astype(np.float32),
        "os": (np.random.uniform(4.0, 16.0, (1, I)) * fi).astype(np.float32),
        "vals": (n((E, T))).astype(np.float32),
        "vsc": (np.random.uniform(0.5, 2.0, (1, I)) / fi).astype(np.float32),
        "offs": striped(idx),
    }


def reference(query, keys_words, keys_scales, cv1, cv2, sres, os, vals, vsc, offs):
    idx = unstriped(offs)
    keysu = unpack_weight(keys_words, keys_scales, "e2m1")
    queryq = mxq(f64(query), 0, "e4m3")
    keysidxg = keysu[:, idx]
    a = queryq.T @ keysidxg
    s = a * f64(cv1)[:1][:, idx] + np.square(a) * f64(cv2)[:1][:, idx]
    p = np.exp(s)
    ptt = p.T
    rg = ptt.reshape(I, K, Q // K).sum(axis=2)
    rv0 = 1.0 / (rg + f64(sres))
    rr = np.repeat(rv0, Q // K, axis=1)
    w0 = ptt * rr
    w = w0.T
    wo1 = w * f64(os)
    wt1 = wo1.T
    vg = f64(vals)[:, idx].reshape(E, H, I // H).mean(axis=2)
    vgr = np.repeat(vg, I // H, axis=1)
    vd = (f64(vals)[:, idx] - vgr) * f64(vsc)
    vt1 = vd.T
    vt1q = mxq(vt1, 0, "e4m3")
    wt1q = mxq(wt1, 0, "e4m3")
    o = vt1q.T @ wt1q
    words, scales = planes(o)
    return o, words, scales

@@ -1,0 +1,271 @@
+from contextlib import ExitStack
+
+import concourse.mybir as mybir
+from concourse.masks import make_identity
+
+D, T, I, Q, E = 512, 2048, 512, 256, 512
+FLOPS = 2 * D * Q * I + 2 * I * E * Q
+BYTES = 4 * D * Q + D * T // 2 + D * T // 32 + 2 * 4 * T + 3 * 4 * I + 4 * E * T + 2 * 128 * (I // 16) + 5 * E * Q + E * Q // 32
+
+F32 = mybir.dt.float32
+BF16 = mybir.dt.bfloat16
+I32 = mybir.dt.int32
+U32 = mybir.dt.uint32
+U16 = mybir.dt.uint16
+U8 = mybir.dt.uint8
+FP8X4 = mybir.dt.float8_e4m3fn_x4
+FP4X4 = mybir.dt.float4_e2m1fn_x4
+ALU = mybir.AluOpType
+ACT = mybir.ActivationFunctionType
+AX = mybir.AxisListType
+
+P = 128
+PACK = 4
+GROUP = 8
+STRETCH = 16
+BANK = 512
+
+
+def tile_attend_owncurve_claimants_centredvalues_pl_kernel(
+    tc, query, keys_words, keys_scales, cv1, cv2, sres, oscale, vals, vsc, offs, out_0, out_1, out_2
+):
+    nc = tc.nc
+    with ExitStack() as ctx:
+        held = ctx.enter_context(tc.tile_pool(name="held", bufs=1))
+        psum = ctx.enter_context(tc.psum_pool(name="psum", bufs=1))
+
+        def sb(name, shape, dtype, tag=None):
+            return held.tile(shape, dtype, name=name, tag=tag or name, align_bytes=64)
+
+        offsets = held.tile([P, I // 16], U16, name="offsets")
+        nc.sync.dma_start(offsets[:], offs)
+
+        key_words = sb("key_words", [P, T], U16)
+        key_bytes = sb("key_bytes", [P, T], U8)
+        nc.vector.memset(key_bytes[:].bitcast(I32), 0)
+        nc.sync.dma_start(key_words[:].bitcast(I32), keys_words[0].bitcast(I32))
+        coef_pool = []
+        for name, src in (("cv1", cv1), ("cv2", cv2)):
+            window = sb(name + "_pool", [P, T], F32)
+            nc.vector.memset(window[0 : P - 1, :].bitcast(I32), 0)
+            nc.scalar.dma_start(window[P - 1 : P, :], src[0:1, :])
+            coef_pool.append(window)
+
+        query_raw = sb("query_raw", [P, PACK, Q], F32)
+        nc.sync.dma_start(query_raw[:], query.rearrange("(p j) q -> p j q", j=PACK))
+        for quad in range(4):
+            nc.sync.dma_start(
+                key_bytes[32 * quad : 32 * quad + 4, :].bitcast(I32),
+                keys_scales[0, 4 * quad : 4 * quad + 4, :].bitcast(I32),
+            )
+        vals_rows = vals.rearrange("(m j) t -> j m t", j=PACK)
+        val_pool = []
+
+        def load_values(j, queue, tag):
+            window = sb("val_pool%d" % j, [P, T], F32, tag)
+            queue.dma_start(window[:], vals_rows[j])
+            val_pool.append(window)
+
+        load_values(0, nc.sync, None)
+
+        ident = sb("ident", [P, P], F32)
+        make_identity(nc, ident[:])
+
+        bytes_listed = sb("bytes_listed", [P, I], U8)
+        nc.vector.tensor_copy(bytes_listed[:], key_bytes[:].indirect(offsets[:]))
+        words_listed = sb("words_listed", [P, I], U16)
+        nc.vector.tensor_copy(words_listed[:], key_words[:].indirect(offsets[:]))
+        bytes_dealt = sb("bytes_dealt", [P, I], U8)
+        nc.vector.tensor_copy(
+            bytes_dealt[:].rearrange("p (r s) -> p r s", r=PACK),
+            bytes_listed[:].rearrange("p (s r) -> p r s", r=PACK),
+        )
+        words_dealt = sb("words_dealt", [P, 2 * I], U8)
+        nc.vector.tensor_copy(
+            words_dealt[:].bitcast(U16).rearrange("p (r s) -> p r s", r=PACK),
+            words_listed[:].rearrange("p (s r) -> p r s", r=PACK),
+        )
+
+        query_bf = sb("query_bf", [P, Q * PACK], BF16)
+        nc.gpsimd.tensor_scalar(
+            query_bf[:].rearrange("p (c i j) -> p c j i", i=4, j=PACK),
+            query_raw[:].rearrange("p j (c i) -> p c j i", i=4),
+            1.0, 0.0, ALU.mult, ALU.add,
+        )
+        query_codes = sb("query_codes", [P, Q], U32)
+        query_scales = sb("query_scales", [P, Q], U8)
+        nc.vector.quantize_mx(query_codes[:].bitcast(FP8X4), query_scales[:], query_bf[:])
+
+        slot_vectors = sb("slot_vectors", [P, 3, 8], F32, "query_raw")
+        val_factor = slot_vectors[:, 0, 0:PACK]
+        reserve = slot_vectors[:, 1, 0:PACK]
+        out_factor = slot_vectors[:, 2, 0:PACK]
+        nc.sync.dma_start(val_factor, vsc.rearrange("o (s r) -> (o s) r", r=PACK))
+        nc.sync.dma_start(reserve, sres.rearrange("(s r) o -> s (r o)", r=PACK))
+        nc.sync.dma_start(out_factor, oscale.rearrange("o (s r) -> (o s) r", r=PACK))
+
+        coef = sb("coef", [P, 2, PACK], F32)
+        for n, window in enumerate(coef_pool):
+            listed = sb("coef_listed%d" % n, [P, I], F32)
+            nc.scalar.activation(listed[:], window[:].indirect(offsets[:]), ACT.Copy)
+            turned = psum.tile([P, PACK, P], F32, name="coef_turned%d" % n, tag="small%d" % n)
+            by_place = listed[:].rearrange("p (s r) -> p r s", r=PACK)
+            for r in range(PACK):
+                nc.tensor.transpose(turned[:, r, :], by_place[:, r, :], ident[:])
+            nc.scalar.copy(coef[:, n, :], turned[:, :, P - 1])
+
+        load_values(1, nc.sync, "cv1_pool")
+        load_values(2, nc.sync, "cv2_pool")
+        load_values(3, nc.sync, "key_words")
+
+        reserve_wide = sb("reserve_wide", [P, P], F32)
+        nc.gpsimd.tensor_copy(
+            reserve_wide[:].rearrange("p (b r i) -> p b r i", r=PACK, i=4),
+            reserve.unsqueeze(1).unsqueeze(3).broadcast_to([P, 8, PACK, 4]),
+        )
+
+        val_codes = [sb("val_codes%d" % j, [P, P], U32) for j in range(PACK)]
+        val_scales = [sb("val_scales%d" % j, [P, P], U8) for j in range(PACK)]
+
+        def values(j):
+            listed = sb("val_listed%d" % j, [P, I], F32, (None, "score1", "cv1_pool", "cv2_pool")[j])
+            nc.scalar.activation(listed[:], val_pool[j][:].indirect(offsets[:]), ACT.Copy)
+            sums = sb("val_sums%d" % j, [P, I // STRETCH], F32, (None, "reserve_wide", "factor", "weight_bf")[j])
+            nc.vector.tensor_reduce(sums[:], listed[:].rearrange("p (h c) -> p h c", c=STRETCH), AX.X, ALU.add)
+            neg_mean = sb("neg_mean%d" % j, [P, P], F32)
+            nc.gpsimd.tensor_scalar(
+                neg_mean[:].rearrange("p (h c) -> p h c", c=4),
+                sums[:].unsqueeze(2).broadcast_to([P, I // STRETCH, 4]),
+                -1.0 / STRETCH, 0.0, ALU.mult, ALU.add,
+            )
+            centred = psum.tile([P, PACK, P], F32, name="centred%d" % j, tag=("centred", "centred", "small0", "small1")[j])
+            by_place = listed[:].rearrange("p (s r) -> p r s", r=PACK)
+            for r in range(PACK):
+                nc.tensor.matmul(centred[:, r, :], by_place[:, r, :], ident[:], start=(r == 0), stop=False, is_transpose=True)
+            for r in range(PACK):
+                nc.tensor.matmul(centred[:, r, :], neg_mean[:], ident[:], start=False, stop=(r == PACK - 1), is_transpose=True)
+            val_bf = sb("val_bf%d" % j, [P, P * PACK], BF16)
+            nc.vector.tensor_tensor(
+                val_bf[:].rearrange("p (e r) -> p e r", r=PACK),
+                centred[:].rearrange("p r e -> p e r"),
+                val_factor.unsqueeze(1).broadcast_to([P, P, PACK]),
+                ALU.mult,
+            )
+            nc.vector.quantize_mx(val_codes[j][:].bitcast(FP8X4), val_scales[j][:], val_bf[:])
+
+        inner = sb("inner", [P, PACK, Q], F32)
+        expo = sb("expo", [P, 64, PACK, 4], F32)
+        prods = []
+        for b in range(2):
+            prod = psum.tile([P, 2, Q], F32, name="prod%d" % b, tag="prod%d" % b)
+            for r2 in range(2):
+                r = 2 * b + r2
+                nc.tensor.matmul_mx(
+                    prod[:, r2, :],
+                    lhsT=words_dealt[:, 2 * P * r : 2 * P * (r + 1)].bitcast(FP4X4),
+                    lhsT_scale=bytes_dealt[:, P * r : P * (r + 1)],
+                    rhs=query_codes[:].bitcast(FP8X4),
+                    rhs_scale=query_scales[:],
+                    start=True, stop=True,
+                )
+            prods.append(prod)
+        values(0)
+        for b in range(2):
+            for r2 in range(2):
+                r = 2 * b + r2
+                nc.scalar.activation(
+                    inner[:, r, :].rearrange("p (u k) -> p u k", u=GROUP),
+                    prods[b][:, r2, :].rearrange("p (k u) -> p u k", u=GROUP),
+                    ACT.Identity, bias=coef[:, 0, r : r + 1], scale=coef[:, 1, r : r + 1],
+                )
+        for b in range(2):
+            score = sb("score%d" % b, [P, 2, Q], F32)
+            nc.vector.tensor_tensor(
+                score[:].rearrange("p r (u k) -> p r u k", u=GROUP),
+                inner[:, 2 * b : 2 * b + 2, :].rearrange("p r (u k) -> p r u k", u=GROUP),
+                prods[b][:].rearrange("p r (k u) -> p r u k", u=GROUP),
+                ALU.mult,
+            )
+            nc.scalar.activation(
+                expo[:, :, 2 * b : 2 * b + 2, :].rearrange("p g r i -> p r g i"),
+                score[:].rearrange("p r (g i) -> p r g i", i=4),
+                ACT.Exp,
+            )
+        expo_flat = expo[:].rearrange("p g r i -> p (g r i)")
+        denom = psum.tile([P, P], F32, name="denom", tag="small0")
+        for u in range(GROUP):
+            nc.tensor.matmul(denom[:], expo_flat[:, P * u : P * (u + 1)], ident[:], start=(u == 0), stop=False, is_transpose=True)
+        nc.tensor.matmul(denom[:], reserve_wide[:], ident[:], start=False, stop=True, is_transpose=True)
+        recip_turned = sb("recip_turned", [P, P], F32)
+        nc.vector.reciprocal(recip_turned[:], denom[:])
+        recip = psum.tile([P, P], F32, name="recip", tag="small1")
+        nc.tensor.transpose(recip[:], recip_turned[:], ident[:])
+        factor = sb("factor", [P, P], F32)
+        nc.vector.tensor_tensor(
+            factor[:].rearrange("p (b r i) -> p b r i", r=PACK, i=4),
+            recip[:].rearrange("p (b r i) -> p b r i", r=PACK, i=4),
+            out_factor.unsqueeze(1).unsqueeze(3).broadcast_to([P, 8, PACK, 4]),
+            ALU.mult,
+        )
+        weight_bf = sb("weight_bf", [P, Q * PACK], BF16)
+        half = Q * PACK // 2
+        for h in range(2):
+            nc.vector.tensor_tensor(
+                weight_bf[:, half * h : half * (h + 1)].rearrange("p (u b i r) -> p u b r i", u=GROUP, i=4, r=PACK),
+                expo_flat.rearrange("p (u h b r i) -> p h u b r i", u=GROUP, h=2, r=PACK, i=4)[:, h],
+                factor[:, 64 * h : 64 * (h + 1)].rearrange("p (b r i) -> p b r i", r=PACK, i=4).unsqueeze(1).broadcast_to([P, GROUP, 4, PACK, 4]),
+                ALU.mult,
+            )
+        weight_codes = sb("weight_codes", [P, Q], U32)
+        weight_scales = sb("weight_scales", [P, Q], U8)
+        nc.vector.quantize_mx(weight_codes[:].bitcast(FP8X4), weight_scales[:], weight_bf[:])
+        values(1)
+        values(2)
+
+        result = sb("result", [P, PACK, Q], F32)
+        sums_out = [psum.tile([P, PACK, P], F32, name="out%d" % h, tag="out%d" % h) for h in range(2)]
+        out_rows = out_0.rearrange("(m j) q -> m j q", j=PACK)
+
+        def product(j):
+            for h in range(2):
+                nc.tensor.matmul_mx(
+                    sums_out[h][:, j, :],
+                    lhsT=val_codes[j][:].bitcast(FP8X4),
+                    lhsT_scale=val_scales[j][:],
+                    rhs=weight_codes[:, P * h : P * (h + 1)].bitcast(FP8X4),
+                    rhs_scale=weight_scales[:, P * h : P * (h + 1)],
+                    start=True, stop=True,
+                )
+
+        def copy_out(j0, j1):
+            for h in range(2):
+                nc.scalar.copy(
+                    result[:, j0:j1, P * h : P * (h + 1)].rearrange("p j (k u) -> p j k u", u=GROUP),
+                    sums_out[h][:, j0:j1, :].rearrange("p j (u k) -> p j k u", u=GROUP),
+                )
+            nc.sync.dma_start(out_rows[:, j0:j1, :], result[:, j0:j1, :])
+
+        for j in range(PACK - 1):
+            product(j)
+        copy_out(0, PACK - 1)
+        values(3)
+        product(3)
+        result_bf = sb("result_bf", [P, Q * PACK], BF16)
+        for h in range(2):
+            dst = result_bf[:, half * h : half * (h + 1)].rearrange("p (k u j) -> p k u j", u=GROUP, j=PACK)
+            src = sums_out[h][:].rearrange("p j (u k) -> p k u j", u=GROUP)
+            if h == 0:
+                nc.vector.tensor_copy(dst, src)
+            else:
+                nc.scalar.copy(dst, src)
+        out_codes = sb("out_codes", [P, Q], U32)
+        out_scales = sb("out_scales", [P, Q], U8)
+        nc.vector.quantize_mx(out_codes[:].bitcast(FP8X4), out_scales[:], result_bf[:])
+        copy_out(PACK - 1, PACK)
+        nc.sync.dma_start(out_1[0].rearrange("p c t -> p (c t)").bitcast(I32), out_codes[:].bitcast(I32))
+        for quad in range(4):
+            queue = nc.scalar if quad % 2 else nc.sync
+            queue.dma_start(
+                out_2[0, 4 * quad : 4 * quad + 4, :].bitcast(I32),
+                out_scales[32 * quad : 32 * quad + 4, :].bitcast(I32),
+            )

@@ -1,7 +1,6 @@
 from contextlib import ExitStack
 
 import concourse.mybir as mybir
-from concourse.masks import make_identity
 
 D, T, I, Q, E = 512, 2048, 512, 256, 512
 FLOPS = 2 * D * Q * I + 2 * I * E * Q
@@ -38,20 +37,31 @@ def tile_attend_owncurve_claimants_centredvalues_pl_kernel(
             return held.tile(shape, dtype, name=name, tag=tag or name, align_bytes=64)
 
         offsets = held.tile([P, I // 16], U16, name="offsets")
-        nc.sync.dma_start(offsets[:], offs)
-
         key_words = sb("key_words", [P, T], U16)
         key_bytes = sb("key_bytes", [P, T], U8)
-        nc.vector.memset(key_bytes[:].bitcast(I32), 0)
-        nc.sync.dma_start(key_words[:].bitcast(I32), keys_words[0].bitcast(I32))
-        coef_pool = []
-        for name, src in (("cv1", cv1), ("cv2", cv2)):
-            window = sb(name + "_pool", [P, T], F32)
-            nc.vector.memset(window[0 : P - 1, :].bitcast(I32), 0)
-            nc.scalar.dma_start(window[P - 1 : P, :], src[0:1, :])
-            coef_pool.append(window)
-
+        coef_pool = [sb(name, [P, T], F32) for name in ("cv1_pool", "cv2_pool")]
         query_raw = sb("query_raw", [P, PACK, Q], F32)
+        zeros = sb("zeros", [P, P], F32)
+        ident = sb("ident", [P, P], F32)
+
+        nc.gpsimd.memset(zeros[:], 0.0)
+        nc.gpsimd.memset(key_bytes[:].bitcast(I32), 0)
+        nc.gpsimd.affine_select(
+            out=ident[:], in_=zeros[:], pattern=[[-1, P]], compare_op=ALU.not_equal, fill=1.0, base=0, channel_multiplier=1
+        )
+        nc.vector.memset(coef_pool[0][0 : P - 1, :].bitcast(I32), 0)
+        nc.gpsimd.memset(coef_pool[1][0 : P - 1, :].bitcast(I32), 0)
+
+        reserve = sb("reserve", [P, PACK], F32)
+        val_factor = sb("val_factor", [P, PACK], F32)
+        out_factor = sb("out_factor", [P, PACK], F32)
+        nc.sync.dma_start(offsets[:], offs)
+        nc.sync.dma_start(reserve[:], sres.rearrange("(s r) o -> s (r o)", r=PACK))
+        nc.sync.dma_start(coef_pool[0][P - 1 : P, :], cv1[0:1, :])
+        nc.sync.dma_start(val_factor[:], vsc.rearrange("o (s r) -> (o s) r", r=PACK))
+        nc.sync.dma_start(out_factor[:], oscale.rearrange("o (s r) -> (o s) r", r=PACK))
+        nc.sync.dma_start(key_words[:].bitcast(I32), keys_words[0].bitcast(I32))
+        nc.sync.dma_start(coef_pool[1][P - 1 : P, :], cv2[0:1, :])
         nc.sync.dma_start(query_raw[:], query.rearrange("(p j) q -> p j q", j=PACK))
         for quad in range(4):
             nc.sync.dma_start(
@@ -61,50 +71,37 @@ def tile_attend_owncurve_claimants_centredvalues_pl_kernel(
         vals_rows = vals.rearrange("(m j) t -> j m t", j=PACK)
         val_pool = []
 
-        def load_values(j, queue, tag):
+        def load_values(j, tag):
             window = sb("val_pool%d" % j, [P, T], F32, tag)
-            queue.dma_start(window[:], vals_rows[j])
+            nc.sync.dma_start(window[:], vals_rows[j])
             val_pool.append(window)
 
-        load_values(0, nc.sync, None)
+        load_values(0, "zeros")
 
-        ident = sb("ident", [P, P], F32)
-        make_identity(nc, ident[:])
+        reserve_wide = sb("reserve_wide", [P, P], F32)
+        nc.scalar.activation(
+            reserve_wide[:].rearrange("p (b r i) -> p b r i", r=PACK, i=4),
+            reserve[:].unsqueeze(1).unsqueeze(3).broadcast_to([P, 8, PACK, 4]),
+            ACT.Copy,
+        )
 
-        bytes_listed = sb("bytes_listed", [P, I], U8)
-        nc.vector.tensor_copy(bytes_listed[:], key_bytes[:].indirect(offsets[:]))
         words_listed = sb("words_listed", [P, I], U16)
         nc.vector.tensor_copy(words_listed[:], key_words[:].indirect(offsets[:]))
-        bytes_dealt = sb("bytes_dealt", [P, I], U8)
-        nc.vector.tensor_copy(
-            bytes_dealt[:].rearrange("p (r s) -> p r s", r=PACK),
-            bytes_listed[:].rearrange("p (s r) -> p r s", r=PACK),
-        )
+        bytes_listed = sb("bytes_listed", [P, I], U8)
+        nc.vector.tensor_copy(bytes_listed[:], key_bytes[:].indirect(offsets[:]))
         words_dealt = sb("words_dealt", [P, 2 * I], U8)
         nc.vector.tensor_copy(
             words_dealt[:].bitcast(U16).rearrange("p (r s) -> p r s", r=PACK),
             words_listed[:].rearrange("p (s r) -> p r s", r=PACK),
         )
-
-        query_bf = sb("query_bf", [P, Q * PACK], BF16)
-        nc.gpsimd.tensor_scalar(
-            query_bf[:].rearrange("p (c i j) -> p c j i", i=4, j=PACK),
-            query_raw[:].rearrange("p j (c i) -> p c j i", i=4),
-            1.0, 0.0, ALU.mult, ALU.add,
+        bytes_dealt = sb("bytes_dealt", [P, I], U8)
+        nc.vector.tensor_copy(
+            bytes_dealt[:].rearrange("p (r s) -> p r s", r=PACK),
+            bytes_listed[:].rearrange("p (s r) -> p r s", r=PACK),
         )
-        query_codes = sb("query_codes", [P, Q], U32)
-        query_scales = sb("query_scales", [P, Q], U8)
-        nc.vector.quantize_mx(query_codes[:].bitcast(FP8X4), query_scales[:], query_bf[:])
 
-        slot_vectors = sb("slot_vectors", [P, 3, 8], F32, "query_raw")
-        val_factor = slot_vectors[:, 0, 0:PACK]
-        reserve = slot_vectors[:, 1, 0:PACK]
-        out_factor = slot_vectors[:, 2, 0:PACK]
-        nc.sync.dma_start(val_factor, vsc.rearrange("o (s r) -> (o s) r", r=PACK))
-        nc.sync.dma_start(reserve, sres.rearrange("(s r) o -> s (r o)", r=PACK))
-        nc.sync.dma_start(out_factor, oscale.rearrange("o (s r) -> (o s) r", r=PACK))
 
-        coef = sb("coef", [P, 2, PACK], F32)
+        turned_coef = []
         for n, window in enumerate(coef_pool):
             listed = sb("coef_listed%d" % n, [P, I], F32)
             nc.scalar.activation(listed[:], window[:].indirect(offsets[:]), ACT.Copy)
@@ -112,85 +109,94 @@ def tile_attend_owncurve_claimants_centredvalues_pl_kernel(
             by_place = listed[:].rearrange("p (s r) -> p r s", r=PACK)
             for r in range(PACK):
                 nc.tensor.transpose(turned[:, r, :], by_place[:, r, :], ident[:])
-            nc.scalar.copy(coef[:, n, :], turned[:, :, P - 1])
+            turned_coef.append(turned)
 
-        load_values(1, nc.sync, "cv1_pool")
-        load_values(2, nc.sync, "cv2_pool")
-        load_values(3, nc.sync, "key_words")
-
-        reserve_wide = sb("reserve_wide", [P, P], F32)
-        nc.gpsimd.tensor_copy(
-            reserve_wide[:].rearrange("p (b r i) -> p b r i", r=PACK, i=4),
-            reserve.unsqueeze(1).unsqueeze(3).broadcast_to([P, 8, PACK, 4]),
+        query_bf = sb("query_bf", [P, Q * PACK], BF16)
+        nc.scalar.copy(
+            query_bf[:].rearrange("p (c i j) -> p c j i", i=4, j=PACK),
+            query_raw[:].rearrange("p j (c i) -> p c j i", i=4),
         )
+        coef = sb("coef", [P, 2, PACK], F32, "query_raw")
+        for n, turned in enumerate(turned_coef):
+            nc.scalar.copy(coef[:, n, :], turned[:, :, P - 1])
+        query_codes = sb("query_codes", [P, Q], U32, "key_bytes")
+        query_scales = sb("query_scales", [P, Q], U8)
+        nc.vector.quantize_mx(query_codes[:].bitcast(FP8X4), query_scales[:], query_bf[:])
+
+        load_values(1, "cv1_pool")
+        load_values(2, "cv2_pool")
+        load_values(3, "key_words")
 
         val_codes = [sb("val_codes%d" % j, [P, P], U32) for j in range(PACK)]
         val_scales = [sb("val_scales%d" % j, [P, P], U8) for j in range(PACK)]
 
-        def values(j):
+        centred_banks = {}
+
+        def centre_values(j):
             listed = sb("val_listed%d" % j, [P, I], F32, (None, "score1", "cv1_pool", "cv2_pool")[j])
             nc.scalar.activation(listed[:], val_pool[j][:].indirect(offsets[:]), ACT.Copy)
-            sums = sb("val_sums%d" % j, [P, I // STRETCH], F32, (None, "reserve_wide", "factor", "weight_bf")[j])
+            sums = sb("val_sums%d" % j, [P, I // STRETCH], F32)
             nc.vector.tensor_reduce(sums[:], listed[:].rearrange("p (h c) -> p h c", c=STRETCH), AX.X, ALU.add)
             neg_mean = sb("neg_mean%d" % j, [P, P], F32)
-            nc.gpsimd.tensor_scalar(
-                neg_mean[:].rearrange("p (h c) -> p h c", c=4),
-                sums[:].unsqueeze(2).broadcast_to([P, I // STRETCH, 4]),
-                -1.0 / STRETCH, 0.0, ALU.mult, ALU.add,
-            )
+            spread_out = neg_mean[:].rearrange("p (h c) -> p h c", c=4)
+            spread_in = sums[:].unsqueeze(2).broadcast_to([P, I // STRETCH, 4])
+            if j < PACK - 1:
+                nc.gpsimd.tensor_scalar(spread_out, spread_in, -1.0 / STRETCH, 0.0, ALU.mult, ALU.add)
+            else:
+                nc.scalar.activation(spread_out, spread_in, ACT.Copy, scale=-1.0 / STRETCH)
             centred = psum.tile([P, PACK, P], F32, name="centred%d" % j, tag=("centred", "centred", "small0", "small1")[j])
             by_place = listed[:].rearrange("p (s r) -> p r s", r=PACK)
             for r in range(PACK):
                 nc.tensor.matmul(centred[:, r, :], by_place[:, r, :], ident[:], start=(r == 0), stop=False, is_transpose=True)
             for r in range(PACK):
                 nc.tensor.matmul(centred[:, r, :], neg_mean[:], ident[:], start=False, stop=(r == PACK - 1), is_transpose=True)
-            val_bf = sb("val_bf%d" % j, [P, P * PACK], BF16)
-            nc.vector.tensor_tensor(
-                val_bf[:].rearrange("p (e r) -> p e r", r=PACK),
-                centred[:].rearrange("p r e -> p e r"),
-                val_factor.unsqueeze(1).broadcast_to([P, P, PACK]),
-                ALU.mult,
-            )
-            nc.vector.quantize_mx(val_codes[j][:].bitcast(FP8X4), val_scales[j][:], val_bf[:])
+            centred_banks[j] = centred
 
-        inner = sb("inner", [P, PACK, Q], F32)
+        def quantise_values(j):
+            centred = centred_banks[j]
+            val_bf = sb("val_bf%d" % j, [P, P, PACK], BF16, (None, "key_words", "weight_bf", None)[j])
+            if j == 1:
+                for r in range(PACK):
+                    nc.scalar.activation(val_bf[:, :, r], centred[:, r, :], ACT.Copy, scale=val_factor[:, r : r + 1])
+            else:
+                nc.vector.tensor_tensor(
+                    val_bf[:],
+                    centred[:].rearrange("p r e -> p e r"),
+                    val_factor[:].unsqueeze(1).broadcast_to([P, P, PACK]),
+                    ALU.mult,
+                )
+            nc.vector.quantize_mx(val_codes[j][:].bitcast(FP8X4), val_scales[j][:], val_bf[:].rearrange("p e r -> p (e r)"))
+
         expo = sb("expo", [P, 64, PACK, 4], F32)
         prods = []
-        for b in range(2):
-            prod = psum.tile([P, 2, Q], F32, name="prod%d" % b, tag="prod%d" % b)
-            for r2 in range(2):
-                r = 2 * b + r2
-                nc.tensor.matmul_mx(
-                    prod[:, r2, :],
-                    lhsT=words_dealt[:, 2 * P * r : 2 * P * (r + 1)].bitcast(FP4X4),
-                    lhsT_scale=bytes_dealt[:, P * r : P * (r + 1)],
-                    rhs=query_codes[:].bitcast(FP8X4),
-                    rhs_scale=query_scales[:],
-                    start=True, stop=True,
-                )
-            prods.append(prod)
-        values(0)
-        for b in range(2):
-            for r2 in range(2):
-                r = 2 * b + r2
-                nc.scalar.activation(
-                    inner[:, r, :].rearrange("p (u k) -> p u k", u=GROUP),
-                    prods[b][:, r2, :].rearrange("p (k u) -> p u k", u=GROUP),
-                    ACT.Identity, bias=coef[:, 0, r : r + 1], scale=coef[:, 1, r : r + 1],
-                )
-        for b in range(2):
-            score = sb("score%d" % b, [P, 2, Q], F32)
-            nc.vector.tensor_tensor(
-                score[:].rearrange("p r (u k) -> p r u k", u=GROUP),
-                inner[:, 2 * b : 2 * b + 2, :].rearrange("p r (u k) -> p r u k", u=GROUP),
-                prods[b][:].rearrange("p r (k u) -> p r u k", u=GROUP),
-                ALU.mult,
+        for r in range(PACK):
+            prod = psum.tile([P, Q], F32, name="prod%d" % r, tag="prod%d" % r)
+            nc.tensor.matmul_mx(
+                prod[:],
+                lhsT=words_dealt[:, 2 * P * r : 2 * P * (r + 1)].bitcast(FP4X4),
+                lhsT_scale=bytes_dealt[:, P * r : P * (r + 1)],
+                rhs=query_codes[:].bitcast(FP8X4),
+                rhs_scale=query_scales[:],
+                start=True, stop=True,
             )
+            prods.append(prod)
+        centre_values(0)
+        inner = sb("inner", [P, PACK, Q], F32, "zeros")
+        scores = [sb("score%d" % b, [P, 2, Q], F32) for b in range(2)]
+        for r in range(PACK):
+            by_member = prods[r][:].rearrange("p (k u) -> p u k", u=GROUP)
+            inner_r = inner[:, r, :].rearrange("p (u k) -> p u k", u=GROUP)
+            nc.scalar.activation(inner_r, by_member, ACT.Identity, bias=coef[:, 0, r : r + 1], scale=coef[:, 1, r : r + 1])
+            nc.vector.tensor_tensor(
+                scores[r // 2][:, r % 2, :].rearrange("p (u k) -> p u k", u=GROUP), inner_r, by_member, ALU.mult
+            )
+        for b in range(2):
             nc.scalar.activation(
                 expo[:, :, 2 * b : 2 * b + 2, :].rearrange("p g r i -> p r g i"),
-                score[:].rearrange("p r (g i) -> p r g i", i=4),
+                scores[b][:].rearrange("p r (g i) -> p r g i", i=4),
                 ACT.Exp,
             )
+        quantise_values(0)
         expo_flat = expo[:].rearrange("p g r i -> p (g r i)")
         denom = psum.tile([P, P], F32, name="denom", tag="small0")
         for u in range(GROUP):
@@ -200,11 +206,13 @@ def tile_attend_owncurve_claimants_centredvalues_pl_kernel(
         nc.vector.reciprocal(recip_turned[:], denom[:])
         recip = psum.tile([P, P], F32, name="recip", tag="small1")
         nc.tensor.transpose(recip[:], recip_turned[:], ident[:])
+        centre_values(1)
+        centre_values(2)
         factor = sb("factor", [P, P], F32)
         nc.vector.tensor_tensor(
             factor[:].rearrange("p (b r i) -> p b r i", r=PACK, i=4),
             recip[:].rearrange("p (b r i) -> p b r i", r=PACK, i=4),
-            out_factor.unsqueeze(1).unsqueeze(3).broadcast_to([P, 8, PACK, 4]),
+            out_factor[:].unsqueeze(1).unsqueeze(3).broadcast_to([P, 8, PACK, 4]),
             ALU.mult,
         )
         weight_bf = sb("weight_bf", [P, Q * PACK], BF16)
@@ -219,52 +227,62 @@ def tile_attend_owncurve_claimants_centredvalues_pl_kernel(
         weight_codes = sb("weight_codes", [P, Q], U32)
         weight_scales = sb("weight_scales", [P, Q], U8)
         nc.vector.quantize_mx(weight_codes[:].bitcast(FP8X4), weight_scales[:], weight_bf[:])
-        values(1)
-        values(2)
+        centre_values(3)
+        for j in range(1, PACK):
+            quantise_values(j)
 
-        result = sb("result", [P, PACK, Q], F32)
-        sums_out = [psum.tile([P, PACK, P], F32, name="out%d" % h, tag="out%d" % h) for h in range(2)]
+        result = sb("result", [P, PACK, Q], F32, "key_words")
+        result_bf = sb("result_bf", [P, Q, PACK], BF16)
         out_rows = out_0.rearrange("(m j) q -> m j q", j=PACK)
-
-        def product(j):
-            for h in range(2):
-                nc.tensor.matmul_mx(
-                    sums_out[h][:, j, :],
-                    lhsT=val_codes[j][:].bitcast(FP8X4),
-                    lhsT_scale=val_scales[j][:],
-                    rhs=weight_codes[:, P * h : P * (h + 1)].bitcast(FP8X4),
-                    rhs_scale=weight_scales[:, P * h : P * (h + 1)],
-                    start=True, stop=True,
-                )
-
-        def copy_out(j0, j1):
-            for h in range(2):
-                nc.scalar.copy(
-                    result[:, j0:j1, P * h : P * (h + 1)].rearrange("p j (k u) -> p j k u", u=GROUP),
-                    sums_out[h][:, j0:j1, :].rearrange("p j (u k) -> p j k u", u=GROUP),
-                )
-            nc.sync.dma_start(out_rows[:, j0:j1, :], result[:, j0:j1, :])
-
-        for j in range(PACK - 1):
-            product(j)
-        copy_out(0, PACK - 1)
-        values(3)
-        product(3)
-        result_bf = sb("result_bf", [P, Q * PACK], BF16)
-        for h in range(2):
-            dst = result_bf[:, half * h : half * (h + 1)].rearrange("p (k u j) -> p k u j", u=GROUP, j=PACK)
-            src = sums_out[h][:].rearrange("p j (u k) -> p k u j", u=GROUP)
-            if h == 0:
-                nc.vector.tensor_copy(dst, src)
-            else:
-                nc.scalar.copy(dst, src)
         out_codes = sb("out_codes", [P, Q], U32)
         out_scales = sb("out_scales", [P, Q], U8)
-        nc.vector.quantize_mx(out_codes[:].bitcast(FP8X4), out_scales[:], result_bf[:])
-        copy_out(PACK - 1, PACK)
+
+        def products(pair, halves):
+            width = Q // halves
+            banks = [
+                psum.tile([P, 2, width], F32, name="out%d%d" % (pair, h), tag="prod%d" % (pair + h)) for h in range(halves)
+            ]
+            for j2 in range(2):
+                for h in range(halves):
+                    cols = slice(width * h, width * (h + 1))
+                    nc.tensor.matmul_mx(
+                        banks[h][:, j2, :],
+                        lhsT=val_codes[2 * pair + j2][:].bitcast(FP8X4),
+                        lhsT_scale=val_scales[2 * pair + j2][:],
+                        rhs=weight_codes[:, cols].bitcast(FP8X4),
+                        rhs_scale=weight_scales[:, cols],
+                        start=True, stop=True,
+                    )
+            return banks
+
+        def round_result(copy, pair, bank, q0):
+            width = bank.shape[2]
+            copy(
+                result_bf[:, q0 : q0 + width, 2 * pair : 2 * pair + 2].rearrange("p (h k u) j -> p h k u j", k=16, u=GROUP),
+                bank[:].rearrange("p j (h u k) -> p h k u j", k=16, u=GROUP),
+            )
+
+        def keep_result(pair, bank, q0):
+            width = bank.shape[2]
+            nc.scalar.copy(
+                result[:, 2 * pair : 2 * pair + 2, q0 : q0 + width].rearrange("p j (h k u) -> p j h k u", k=16, u=GROUP),
+                bank[:].rearrange("p j (h u k) -> p j h k u", k=16, u=GROUP),
+            )
+
+        first = products(0, 1)
+        round_result(nc.scalar.copy, 0, first[0], 0)
+        keep_result(0, first[0], 0)
+        nc.scalar.dma_start(out_rows[:, 0:2, :], result[:, 0:2, :])
+        last = products(1, 2)
+        round_result(nc.vector.tensor_copy, 1, last[0], 0)
+        round_result(nc.scalar.copy, 1, last[1], P)
+        nc.vector.quantize_mx(out_codes[:].bitcast(FP8X4), out_scales[:], result_bf[:].rearrange("p q j -> p (q j)"))
+        keep_result(1, last[1], P)
+        keep_result(1, last[0], 0)
+        nc.scalar.dma_start(out_rows[:, 2:4, :], result[:, 2:4, :])
         nc.sync.dma_start(out_1[0].rearrange("p c t -> p (c t)").bitcast(I32), out_codes[:].bitcast(I32))
         for quad in range(4):
-            queue = nc.scalar if quad % 2 else nc.sync
+            queue = nc.sync if quad < 3 else nc.scalar
             queue.dma_start(
                 out_2[0, 4 * quad : 4 * quad + 4, :].bitcast(I32),
                 out_scales[32 * quad : 32 * quad + 4, :].bitcast(I32),

@@ -123,9 +123,9 @@ def tile_attend_owncurve_claimants_centredvalues_pl_kernel(
         query_scales = sb("query_scales", [P, Q], U8)
         nc.vector.quantize_mx(query_codes[:].bitcast(FP8X4), query_scales[:], query_bf[:])
 
-        load_values(1, "cv1_pool")
-        load_values(2, "cv2_pool")
-        load_values(3, "key_words")
+        load_values(1, "key_words")
+        load_values(2, "cv1_pool")
+        load_values(3, "cv2_pool")
 
         val_codes = [sb("val_codes%d" % j, [P, P], U32) for j in range(PACK)]
         val_scales = [sb("val_scales%d" % j, [P, P], U8) for j in range(PACK)]
@@ -133,7 +133,7 @@ def tile_attend_owncurve_claimants_centredvalues_pl_kernel(
         centred_banks = {}
 
         def centre_values(j):
-            listed = sb("val_listed%d" % j, [P, I], F32, (None, "score1", "cv1_pool", "cv2_pool")[j])
+            listed = sb("val_listed%d" % j, [P, I], F32, (None, "score1", "key_words", "cv1_pool")[j])
             nc.scalar.activation(listed[:], val_pool[j][:].indirect(offsets[:]), ACT.Copy)
             sums = sb("val_sums%d" % j, [P, I // STRETCH], F32)
             nc.vector.tensor_reduce(sums[:], listed[:].rearrange("p (h c) -> p h c", c=STRETCH), AX.X, ALU.add)
@@ -154,7 +154,7 @@ def tile_attend_owncurve_claimants_centredvalues_pl_kernel(
 
         def quantise_values(j):
             centred = centred_banks[j]
-            val_bf = sb("val_bf%d" % j, [P, P, PACK], BF16, (None, "key_words", "weight_bf", None)[j])
+            val_bf = sb("val_bf%d" % j, [P, P, PACK], BF16, (None, "cv2_pool", "weight_bf", None)[j])
             if j == 1:
                 for r in range(PACK):
                     nc.scalar.activation(val_bf[:, :, r], centred[:, r, :], ACT.Copy, scale=val_factor[:, r : r + 1])
@@ -231,7 +231,7 @@ def tile_attend_owncurve_claimants_centredvalues_pl_kernel(
         for j in range(1, PACK):
             quantise_values(j)
 
-        result = sb("result", [P, PACK, Q], F32, "key_words")
+        result = sb("result", [P, PACK, Q], F32, "cv2_pool")
         result_bf = sb("result_bf", [P, Q, PACK], BF16)
         out_rows = out_0.rearrange("(m j) q -> m j q", j=PACK)
         out_codes = sb("out_codes", [P, Q], U32)
@@ -262,23 +262,23 @@ def tile_attend_owncurve_claimants_centredvalues_pl_kernel(
                 bank[:].rearrange("p j (h u k) -> p h k u j", k=16, u=GROUP),
             )
 
-        def keep_result(pair, bank, q0):
+        def keep_result(copy, pair, bank, q0):
             width = bank.shape[2]
-            nc.scalar.copy(
+            copy(
                 result[:, 2 * pair : 2 * pair + 2, q0 : q0 + width].rearrange("p j (h k u) -> p j h k u", k=16, u=GROUP),
                 bank[:].rearrange("p j (h u k) -> p j h k u", k=16, u=GROUP),
             )
 
         first = products(0, 1)
         round_result(nc.scalar.copy, 0, first[0], 0)
-        keep_result(0, first[0], 0)
+        keep_result(nc.scalar.copy, 0, first[0], 0)
         nc.scalar.dma_start(out_rows[:, 0:2, :], result[:, 0:2, :])
         last = products(1, 2)
         round_result(nc.vector.tensor_copy, 1, last[0], 0)
         round_result(nc.scalar.copy, 1, last[1], P)
+        keep_result(nc.vector.tensor_copy, 1, last[0], 0)
+        keep_result(nc.scalar.copy, 1, last[1], P)
         nc.vector.quantize_mx(out_codes[:].bitcast(FP8X4), out_scales[:], result_bf[:].rearrange("p q j -> p (q j)"))
-        keep_result(1, last[1], P)
-        keep_result(1, last[0], 0)
         nc.scalar.dma_start(out_rows[:, 2:4, :], result[:, 2:4, :])
         nc.sync.dma_start(out_1[0].rearrange("p c t -> p (c t)").bitcast(I32), out_codes[:].bitcast(I32))
         for quad in range(4):

@@ -135,7 +135,7 @@ def tile_attend_owncurve_claimants_centredvalues_pl_kernel(
         def centre_values(j):
             listed = sb("val_listed%d" % j, [P, I], F32, (None, "score1", "key_words", "cv1_pool")[j])
             nc.scalar.activation(listed[:], val_pool[j][:].indirect(offsets[:]), ACT.Copy)
-            sums = sb("val_sums%d" % j, [P, I // STRETCH], F32)
+            sums = sb("val_sums%d" % j, [P, I // STRETCH], F32, "reserve_wide" if j == 1 else None)
             nc.vector.tensor_reduce(sums[:], listed[:].rearrange("p (h c) -> p h c", c=STRETCH), AX.X, ALU.add)
             neg_mean = sb("neg_mean%d" % j, [P, P], F32)
             spread_out = neg_mean[:].rearrange("p (h c) -> p h c", c=4)
@@ -190,10 +190,10 @@ def tile_attend_owncurve_claimants_centredvalues_pl_kernel(
             nc.vector.tensor_tensor(
                 scores[r // 2][:, r % 2, :].rearrange("p (u k) -> p u k", u=GROUP), inner_r, by_member, ALU.mult
             )
-        for b in range(2):
+        for b, runs in ((0, slice(0, 64)), (1, slice(0, 32)), (1, slice(32, 64))):
             nc.scalar.activation(
-                expo[:, :, 2 * b : 2 * b + 2, :].rearrange("p g r i -> p r g i"),
-                scores[b][:].rearrange("p r (g i) -> p r g i", i=4),
+                expo[:, runs, 2 * b : 2 * b + 2, :].rearrange("p g r i -> p r g i"),
+                scores[b][:].rearrange("p r (g i) -> p r g i", i=4)[:, :, runs, :],
                 ACT.Exp,
             )
         quantise_values(0)
@@ -282,7 +282,7 @@ def tile_attend_owncurve_claimants_centredvalues_pl_kernel(
         nc.scalar.dma_start(out_rows[:, 2:4, :], result[:, 2:4, :])
         nc.sync.dma_start(out_1[0].rearrange("p c t -> p (c t)").bitcast(I32), out_codes[:].bitcast(I32))
         for quad in range(4):
-            queue = nc.sync if quad < 3 else nc.scalar
+            queue = nc.sync if quad < 2 else nc.scalar
             queue.dma_start(
                 out_2[0, 4 * quad : 4 * quad + 4, :].bitcast(I32),
                 out_scales[32 * quad : 32 * quad + 4, :].bitcast(I32),

@@ -154,17 +154,13 @@ def tile_attend_owncurve_claimants_centredvalues_pl_kernel(
 
         def quantise_values(j):
             centred = centred_banks[j]
-            val_bf = sb("val_bf%d" % j, [P, P, PACK], BF16, (None, "cv2_pool", "weight_bf", None)[j])
-            if j == 1:
-                for r in range(PACK):
-                    nc.scalar.activation(val_bf[:, :, r], centred[:, r, :], ACT.Copy, scale=val_factor[:, r : r + 1])
-            else:
-                nc.vector.tensor_tensor(
-                    val_bf[:],
-                    centred[:].rearrange("p r e -> p e r"),
-                    val_factor[:].unsqueeze(1).broadcast_to([P, P, PACK]),
-                    ALU.mult,
-                )
+            val_bf = sb("val_bf%d" % j, [P, P, PACK], BF16, "weight_bf" if j == 2 else None)
+            nc.vector.tensor_tensor(
+                val_bf[:],
+                centred[:].rearrange("p r e -> p e r"),
+                val_factor[:].unsqueeze(1).broadcast_to([P, P, PACK]),
+                ALU.mult,
+            )
             nc.vector.quantize_mx(val_codes[j][:].bitcast(FP8X4), val_scales[j][:], val_bf[:].rearrange("p e r -> p (e r)"))
 
         expo = sb("expo", [P, 64, PACK, 4], F32)

from contextlib import ExitStack

import concourse.mybir as mybir

D, T, I, Q, E = 512, 2048, 512, 256, 512
FLOPS = 2 * D * Q * I + 2 * I * E * Q
BYTES = 4 * D * Q + D * T // 2 + D * T // 32 + 2 * 4 * T + 3 * 4 * I + 4 * E * T + 2 * 128 * (I // 16) + 5 * E * Q + E * Q // 32

F32 = mybir.dt.float32
BF16 = mybir.dt.bfloat16
I32 = mybir.dt.int32
U32 = mybir.dt.uint32
U16 = mybir.dt.uint16
U8 = mybir.dt.uint8
FP8X4 = mybir.dt.float8_e4m3fn_x4
FP4X4 = mybir.dt.float4_e2m1fn_x4
ALU = mybir.AluOpType
ACT = mybir.ActivationFunctionType
AX = mybir.AxisListType

P = 128
PACK = 4
GROUP = 8
STRETCH = 16
BANK = 512


def tile_attend_owncurve_claimants_centredvalues_pl_kernel(
    tc, query, keys_words, keys_scales, cv1, cv2, sres, oscale, vals, vsc, offs, out_0, out_1, out_2
):
    nc = tc.nc
    with ExitStack() as ctx:
        held = ctx.enter_context(tc.tile_pool(name="held", bufs=1))
        psum = ctx.enter_context(tc.psum_pool(name="psum", bufs=1))

        def sb(name, shape, dtype, tag=None):
            return held.tile(shape, dtype, name=name, tag=tag or name, align_bytes=64)

        offsets = held.tile([P, I // 16], U16, name="offsets")
        key_words = sb("key_words", [P, T], U16)
        key_bytes = sb("key_bytes", [P, T], U8)
        coef_pool = [sb(name, [P, T], F32) for name in ("cv1_pool", "cv2_pool")]
        query_raw = sb("query_raw", [P, PACK, Q], F32)
        zeros = sb("zeros", [P, P], F32)
        ident = sb("ident", [P, P], F32)

        nc.gpsimd.memset(zeros[:], 0.0)
        nc.gpsimd.memset(key_bytes[:].bitcast(I32), 0)
        nc.gpsimd.affine_select(
            out=ident[:], in_=zeros[:], pattern=[[-1, P]], compare_op=ALU.not_equal, fill=1.0, base=0, channel_multiplier=1
        )
        nc.vector.memset(coef_pool[0][0 : P - 1, :].bitcast(I32), 0)
        nc.gpsimd.memset(coef_pool[1][0 : P - 1, :].bitcast(I32), 0)

        reserve = sb("reserve", [P, PACK], F32)
        val_factor = sb("val_factor", [P, PACK], F32)
        out_factor = sb("out_factor", [P, PACK], F32)
        nc.sync.dma_start(offsets[:], offs)
        nc.sync.dma_start(reserve[:], sres.rearrange("(s r) o -> s (r o)", r=PACK))
        nc.sync.dma_start(coef_pool[0][P - 1 : P, :], cv1[0:1, :])
        nc.sync.dma_start(val_factor[:], vsc.rearrange("o (s r) -> (o s) r", r=PACK))
        nc.sync.dma_start(out_factor[:], oscale.rearrange("o (s r) -> (o s) r", r=PACK))
        nc.sync.dma_start(key_words[:].bitcast(I32), keys_words[0].bitcast(I32))
        nc.sync.dma_start(coef_pool[1][P - 1 : P, :], cv2[0:1, :])
        nc.sync.dma_start(query_raw[:], query.rearrange("(p j) q -> p j q", j=PACK))
        for quad in range(4):
            nc.sync.dma_start(
                key_bytes[32 * quad : 32 * quad + 4, :].bitcast(I32),
                keys_scales[0, 4 * quad : 4 * quad + 4, :].bitcast(I32),
            )
        vals_rows = vals.rearrange("(m j) t -> j m t", j=PACK)
        val_pool = []

        def load_values(j, tag):
            window = sb("val_pool%d" % j, [P, T], F32, tag)
            nc.sync.dma_start(window[:], vals_rows[j])
            val_pool.append(window)

        load_values(0, "zeros")

        reserve_wide = sb("reserve_wide", [P, P], F32)
        nc.scalar.activation(
            reserve_wide[:].rearrange("p (b r i) -> p b r i", r=PACK, i=4),
            reserve[:].unsqueeze(1).unsqueeze(3).broadcast_to([P, 8, PACK, 4]),
            ACT.Copy,
        )

        words_listed = sb("words_listed", [P, I], U16)
        nc.vector.tensor_copy(words_listed[:], key_words[:].indirect(offsets[:]))
        bytes_listed = sb("bytes_listed", [P, I], U8)
        nc.vector.tensor_copy(bytes_listed[:], key_bytes[:].indirect(offsets[:]))
        words_dealt = sb("words_dealt", [P, 2 * I], U8)
        nc.vector.tensor_copy(
            words_dealt[:].bitcast(U16).rearrange("p (r s) -> p r s", r=PACK),
            words_listed[:].rearrange("p (s r) -> p r s", r=PACK),
        )
        bytes_dealt = sb("bytes_dealt", [P, I], U8)
        nc.vector.tensor_copy(
            bytes_dealt[:].rearrange("p (r s) -> p r s", r=PACK),
            bytes_listed[:].rearrange("p (s r) -> p r s", r=PACK),
        )


        turned_coef = []
        for n, window in enumerate(coef_pool):
            listed = sb("coef_listed%d" % n, [P, I], F32)
            nc.scalar.activation(listed[:], window[:].indirect(offsets[:]), ACT.Copy)
            turned = psum.tile([P, PACK, P], F32, name="coef_turned%d" % n, tag="small%d" % n)
            by_place = listed[:].rearrange("p (s r) -> p r s", r=PACK)
            for r in range(PACK):
                nc.tensor.transpose(turned[:, r, :], by_place[:, r, :], ident[:])
            turned_coef.append(turned)

        query_bf = sb("query_bf", [P, Q * PACK], BF16)
        nc.scalar.copy(
            query_bf[:].rearrange("p (c i j) -> p c j i", i=4, j=PACK),
            query_raw[:].rearrange("p j (c i) -> p c j i", i=4),
        )
        coef = sb("coef", [P, 2, PACK], F32, "query_raw")
        for n, turned in enumerate(turned_coef):
            nc.scalar.copy(coef[:, n, :], turned[:, :, P - 1])
        query_codes = sb("query_codes", [P, Q], U32, "key_bytes")
        query_scales = sb("query_scales", [P, Q], U8)
        nc.vector.quantize_mx(query_codes[:].bitcast(FP8X4), query_scales[:], query_bf[:])

        load_values(1, "key_words")
        load_values(2, "cv1_pool")
        load_values(3, "cv2_pool")

        val_codes = [sb("val_codes%d" % j, [P, P], U32) for j in range(PACK)]
        val_scales = [sb("val_scales%d" % j, [P, P], U8) for j in range(PACK)]

        centred_banks = {}

        def centre_values(j):
            listed = sb("val_listed%d" % j, [P, I], F32, (None, "score1", "key_words", "cv1_pool")[j])
            nc.scalar.activation(listed[:], val_pool[j][:].indirect(offsets[:]), ACT.Copy)
            sums = sb("val_sums%d" % j, [P, I // STRETCH], F32, "reserve_wide" if j == 1 else None)
            nc.vector.tensor_reduce(sums[:], listed[:].rearrange("p (h c) -> p h c", c=STRETCH), AX.X, ALU.add)
            neg_mean = sb("neg_mean%d" % j, [P, P], F32)
            spread_out = neg_mean[:].rearrange("p (h c) -> p h c", c=4)
            spread_in = sums[:].unsqueeze(2).broadcast_to([P, I // STRETCH, 4])
            if j < PACK - 1:
                nc.gpsimd.tensor_scalar(spread_out, spread_in, -1.0 / STRETCH, 0.0, ALU.mult, ALU.add)
            else:
                nc.scalar.activation(spread_out, spread_in, ACT.Copy, scale=-1.0 / STRETCH)
            centred = psum.tile([P, PACK, P], F32, name="centred%d" % j, tag=("centred", "centred", "small0", "small1")[j])
            by_place = listed[:].rearrange("p (s r) -> p r s", r=PACK)
            for r in range(PACK):
                nc.tensor.matmul(centred[:, r, :], by_place[:, r, :], ident[:], start=(r == 0), stop=False, is_transpose=True)
            for r in range(PACK):
                nc.tensor.matmul(centred[:, r, :], neg_mean[:], ident[:], start=False, stop=(r == PACK - 1), is_transpose=True)
            centred_banks[j] = centred

        def quantise_values(j):
            centred = centred_banks[j]
            val_bf = sb("val_bf%d" % j, [P, P, PACK], BF16, "weight_bf" if j == 2 else None)
            nc.vector.tensor_tensor(
                val_bf[:],
                centred[:].rearrange("p r e -> p e r"),
                val_factor[:].unsqueeze(1).broadcast_to([P, P, PACK]),
                ALU.mult,
            )
            nc.vector.quantize_mx(val_codes[j][:].bitcast(FP8X4), val_scales[j][:], val_bf[:].rearrange("p e r -> p (e r)"))

        expo = sb("expo", [P, 64, PACK, 4], F32)
        prods = []
        for r in range(PACK):
            prod = psum.tile([P, Q], F32, name="prod%d" % r, tag="prod%d" % r)
            nc.tensor.matmul_mx(
                prod[:],
                lhsT=words_dealt[:, 2 * P * r : 2 * P * (r + 1)].bitcast(FP4X4),
                lhsT_scale=bytes_dealt[:, P * r : P * (r + 1)],
                rhs=query_codes[:].bitcast(FP8X4),
                rhs_scale=query_scales[:],
                start=True, stop=True,
            )
            prods.append(prod)
        centre_values(0)
        inner = sb("inner", [P, PACK, Q], F32, "zeros")
        scores = [sb("score%d" % b, [P, 2, Q], F32) for b in range(2)]
        for r in range(PACK):
            by_member = prods[r][:].rearrange("p (k u) -> p u k", u=GROUP)
            inner_r = inner[:, r, :].rearrange("p (u k) -> p u k", u=GROUP)
            nc.scalar.activation(inner_r, by_member, ACT.Identity, bias=coef[:, 0, r : r + 1], scale=coef[:, 1, r : r + 1])
            nc.vector.tensor_tensor(
                scores[r // 2][:, r % 2, :].rearrange("p (u k) -> p u k", u=GROUP), inner_r, by_member, ALU.mult
            )
        for b, runs in ((0, slice(0, 64)), (1, slice(0, 32)), (1, slice(32, 64))):
            nc.scalar.activation(
                expo[:, runs, 2 * b : 2 * b + 2, :].rearrange("p g r i -> p r g i"),
                scores[b][:].rearrange("p r (g i) -> p r g i", i=4)[:, :, runs, :],
                ACT.Exp,
            )
        quantise_values(0)
        expo_flat = expo[:].rearrange("p g r i -> p (g r i)")
        denom = psum.tile([P, P], F32, name="denom", tag="small0")
        for u in range(GROUP):
            nc.tensor.matmul(denom[:], expo_flat[:, P * u : P * (u + 1)], ident[:], start=(u == 0), stop=False, is_transpose=True)
        nc.tensor.matmul(denom[:], reserve_wide[:], ident[:], start=False, stop=True, is_transpose=True)
        recip_turned = sb("recip_turned", [P, P], F32)
        nc.vector.reciprocal(recip_turned[:], denom[:])
        recip = psum.tile([P, P], F32, name="recip", tag="small1")
        nc.tensor.transpose(recip[:], recip_turned[:], ident[:])
        centre_values(1)
        centre_values(2)
        factor = sb("factor", [P, P], F32)
        nc.vector.tensor_tensor(
            factor[:].rearrange("p (b r i) -> p b r i", r=PACK, i=4),
            recip[:].rearrange("p (b r i) -> p b r i", r=PACK, i=4),
            out_factor[:].unsqueeze(1).unsqueeze(3).broadcast_to([P, 8, PACK, 4]),
            ALU.mult,
        )
        weight_bf = sb("weight_bf", [P, Q * PACK], BF16)
        half = Q * PACK // 2
        for h in range(2):
            nc.vector.tensor_tensor(
                weight_bf[:, half * h : half * (h + 1)].rearrange("p (u b i r) -> p u b r i", u=GROUP, i=4, r=PACK),
                expo_flat.rearrange("p (u h b r i) -> p h u b r i", u=GROUP, h=2, r=PACK, i=4)[:, h],
                factor[:, 64 * h : 64 * (h + 1)].rearrange("p (b r i) -> p b r i", r=PACK, i=4).unsqueeze(1).broadcast_to([P, GROUP, 4, PACK, 4]),
                ALU.mult,
            )
        weight_codes = sb("weight_codes", [P, Q], U32)
        weight_scales = sb("weight_scales", [P, Q], U8)
        nc.vector.quantize_mx(weight_codes[:].bitcast(FP8X4), weight_scales[:], weight_bf[:])
        centre_values(3)
        for j in range(1, PACK):
            quantise_values(j)

        result = sb("result", [P, PACK, Q], F32, "cv2_pool")
        result_bf = sb("result_bf", [P, Q, PACK], BF16)
        out_rows = out_0.rearrange("(m j) q -> m j q", j=PACK)
        out_codes = sb("out_codes", [P, Q], U32)
        out_scales = sb("out_scales", [P, Q], U8)

        def products(pair, halves):
            width = Q // halves
            banks = [
                psum.tile([P, 2, width], F32, name="out%d%d" % (pair, h), tag="prod%d" % (pair + h)) for h in range(halves)
            ]
            for j2 in range(2):
                for h in range(halves):
                    cols = slice(width * h, width * (h + 1))
                    nc.tensor.matmul_mx(
                        banks[h][:, j2, :],
                        lhsT=val_codes[2 * pair + j2][:].bitcast(FP8X4),
                        lhsT_scale=val_scales[2 * pair + j2][:],
                        rhs=weight_codes[:, cols].bitcast(FP8X4),
                        rhs_scale=weight_scales[:, cols],
                        start=True, stop=True,
                    )
            return banks

        def round_result(copy, pair, bank, q0):
            width = bank.shape[2]
            copy(
                result_bf[:, q0 : q0 + width, 2 * pair : 2 * pair + 2].rearrange("p (h k u) j -> p h k u j", k=16, u=GROUP),
                bank[:].rearrange("p j (h u k) -> p h k u j", k=16, u=GROUP),
            )

        def keep_result(copy, pair, bank, q0):
            width = bank.shape[2]
            copy(
                result[:, 2 * pair : 2 * pair + 2, q0 : q0 + width].rearrange("p j (h k u) -> p j h k u", k=16, u=GROUP),
                bank[:].rearrange("p j (h u k) -> p j h k u", k=16, u=GROUP),
            )

        first = products(0, 1)
        round_result(nc.scalar.copy, 0, first[0], 0)
        keep_result(nc.scalar.copy, 0, first[0], 0)
        nc.scalar.dma_start(out_rows[:, 0:2, :], result[:, 0:2, :])
        last = products(1, 2)
        round_result(nc.vector.tensor_copy, 1, last[0], 0)
        round_result(nc.scalar.copy, 1, last[1], P)
        keep_result(nc.vector.tensor_copy, 1, last[0], 0)
        keep_result(nc.scalar.copy, 1, last[1], P)
        nc.vector.quantize_mx(out_codes[:].bitcast(FP8X4), out_scales[:], result_bf[:].rearrange("p q j -> p (q j)"))
        nc.scalar.dma_start(out_rows[:, 2:4, :], result[:, 2:4, :])
        nc.sync.dma_start(out_1[0].rearrange("p c t -> p (c t)").bitcast(I32), out_codes[:].bitcast(I32))
        for quad in range(4):
            queue = nc.sync if quad < 2 else nc.scalar
            queue.dma_start(
                out_2[0, 4 * quad : 4 * quad + 4, :].bitcast(I32),
                out_scales[32 * quad : 32 * quad + 4, :].bitcast(I32),
            )
